import numpy as np, ml_dtypes
CORES = [16,23,24,31,64,71]
N = 6
KT, FB, TK = 2, 128, 256
def setup_inputs(rng):
    return {"x": rng.standard_normal((N, 128, KT * TK), dtype=np.float32).astype(ml_dtypes.bfloat16), "w": rng.standard_normal((N, 128, KT * N * FB), dtype=np.float32).astype(ml_dtypes.bfloat16)}
def setup_inputs_big(rng):
    d = setup_inputs(rng)
    for k in ("x", "w"): d[k] = (d[k].astype(np.float32) * 1024.0).astype(d[k].dtype)
    return d
def setup_inputs_small(rng):
    d = setup_inputs(rng)
    for k in ("x", "w"): d[k] = (d[k].astype(np.float32) * (1 / 1024.0)).astype(d[k].dtype)
    return d
def setup_inputs_apart(rng):
    d = setup_inputs(rng)
    f = (10.0 ** rng.permutation(np.linspace(-1.5, 1.5, N))).astype(np.float32).reshape(N, 1, 1)
    for k in ("x", "w"): d[k] = (d[k].astype(np.float32) * f).astype(d[k].dtype)
    return d
def reference(x, w):
    X, W = x.astype(np.float64), w.astype(np.float64)
    y = np.zeros((N, FB, N * TK))
    for j in range(N):
        for r in range(N):
            for t in range(KT):
                y[r][:, TK * j:TK * j + TK] += W[j][:, FB * (N * t + r):FB * (N * t + r) + FB].T @ X[j][:, TK * t:TK * t + TK]
    return {"y": y.astype(ml_dtypes.bfloat16 if x.dtype != np.float64 else np.float64)}

@@ -1,0 +1,269 @@
+from concourse.bass import DstId, RemoteDMATransfer
+
+N, KT, FB, TK = 6, 2, 128, 256
+SIM_CORES = 80
+SLOTS = 4
+
+RELAY = "helper"
+FAR_VIA_PLANE = False
+STAGE = False
+HOME_FIRST = False
+SPLIT_LOAD = True
+N_HOP1 = 4
+N_FWD = 4
+N_HOME = 8
+N_DIRECT = 4
+SPREAD = True
+
+SCRATCH = {
+    "xs": ("sbuf", [128, KT * TK], "bfloat16"),
+    "ws": ("sbuf", [128, KT * N * FB], "bfloat16"),
+    "out": ("sbuf", [128, N * TK], "bfloat16"),
+    "land": ("sbuf", [128, N * TK], "bfloat16"),
+    "stage": ("dram", [N, 128, TK], "bfloat16"),
+    "relay": ("dram", [SLOTS, 128, TK], "bfloat16"),
+    "dland": ("dram", [N, 128, TK], "bfloat16"),
+}
+for _i in range(N):
+    SCRATCH["ps%d" % _i] = ("psum", [128, 512], "float32")
+
+SEMAPHORES = (["ldx", "ldw0", "ldw1", "sent", "st"] + ["mm%d" % i for i in range(N)] + ["cp%d" % i for i in range(N)]
+              + ["sg%d" % i for i in range(4)] + ["a%d" % i for i in range(N)] + ["r%d" % i for i in range(SLOTS)])
+
+
+def _bits(m):
+    return [b for b in range(m.bit_length()) if (m >> b) & 1]
+
+
+def _pow2(n):
+    p = 1
+    while p * 2 <= n:
+        p *= 2
+    return p
+
+
+def _engine_sets(core, topo):
+    every, some = ~0, 0
+    for c in range(SIM_CORES):
+        if c != core:
+            every &= topo.mask(core, c)
+            some |= topo.mask(core, c)
+    return _bits(every), _bits(some & ~every)
+
+
+def _relays(s, dsts, cores, topo, links, nth):
+    cs, cd = topo.chip(s), topo.chip(dsts[0])
+
+    def fits(h):
+        return h != s and topo.may_write(s, h) and all(topo.may_write(h, d) for d in dsts)
+
+    if FAR_VIA_PLANE and links == 2:
+        got = [h for h in range(SIM_CORES) if h not in cores and fits(h) and topo.same_plane(cs, topo.chip(h))
+               and topo.mates(topo.chip(h), cd) and topo.die(h) == topo.die(s)]
+        if got:
+            return got
+    if RELAY == "sibling" or (RELAY == "mixed" and nth > 0):
+        got = [h for h in cores if topo.chip(h) == cs and fits(h)]
+        if got:
+            return got
+    return [h for h in range(SIM_CORES) if h not in cores and fits(h) and topo.chip(h) == cs
+            and topo.die(h) == topo.die(s)]
+
+
+def _deal(core, call, topo):
+    caps = {"hop1": N_HOP1, "fwd": N_FWD, "home": N_HOME, "direct": N_DIRECT}
+    narrow, upper = _engine_sets(core, topo)
+    for pool, inside in ((upper or narrow, True), (narrow, False)):
+        part = [t for t in call if (topo.chip(t["to"]) == topo.chip(core)) == inside]
+        if not part:
+            continue
+        if SPREAD:
+            pool = pool[0::2] + pool[1::2]
+        n = _pow2(len(pool) // len(part))
+        at = 0
+        for t in part:
+            k = min(n, caps[t["kind"]])
+            t["eng"] = pool[at:at + k]
+            at += k
+
+
+def _plan(cores, topo):
+    own, fwd, seqs, slots = {}, {}, [], {}
+    arrive = [dict() for _ in cores]
+    for j, s in enumerate(cores):
+        cs = topo.chip(s)
+        groups = {}
+        for r, d in enumerate(cores):
+            if r != j:
+                groups.setdefault(topo.chip(d), []).append(r)
+        home = groups.pop(cs, [])
+
+        def links(ch):
+            return 1 if (topo.mates(cs, ch) or topo.same_plane(cs, ch)) else 2
+
+        def free(rs):
+            return all(topo.may_write(s, cores[r]) for r in rs)
+
+        away = sorted(groups.items(), key=lambda kv: (free(kv[1]), -links(kv[0])))
+        calls = []
+        homes = [dict(to=cores[r], src=("out", r), dst=("land", j), sem="a%d" % j, kind="home", blk=r, far=0)
+                 for r in home]
+        early = HOME_FIRST and homes and all(free(rs) for _, rs in away)
+        if early:
+            calls.append(homes)
+        for ch, rs in away:
+            call = []
+            if free(rs):
+                long = STAGE is True or (STAGE == "later" and len(calls) > 0)
+                for r in rs:
+                    call.append(dict(to=cores[r], src=("stage" if long else "out", r),
+                                     dst=("dland" if long else "land", j), sem="a%d" % j, kind="direct", blk=r,
+                                     far=links(ch)))
+            else:
+                hs = _relays(s, [cores[r] for r in rs], cores, topo, links(ch), len(calls))
+                batch = {}
+                for i, r in enumerate(rs):
+                    h = hs[i % len(hs)]
+                    k = slots.get(h, 0)
+                    slots[h] = k + 1
+                    if h not in batch:
+                        batch[h] = ("r%d" % k, [], [])
+                    sem, ins, outs = batch[h]
+                    t = dict(to=h, src=("out", r), dst=("relay", k), sem=sem, kind="hop1", blk=r)
+                    call.append(t)
+                    ins.append(t)
+                    outs.append(dict(to=cores[r], src=("relay", k), dst=("dland", j), sem="a%d" % j, kind="fwd",
+                                     blk=r, late=(1, len(calls), links(ch))))
+                for h, b in batch.items():
+                    fwd.setdefault(h, []).append(b)
+            calls.append(call)
+        if not early:
+            for t in homes:
+                if calls and all(topo.chip(u["to"]) != cs for u in calls[-1]):
+                    calls[-1].append(t)
+                else:
+                    calls.append([t])
+        pos = {t["blk"]: i for i, t in enumerate(t for call in calls for t in call)}
+        own[s] = []
+        for i, call in enumerate(calls):
+            _deal(s, call, topo)
+            waits = [("cp%d" % pos[t["blk"]], 1) for t in call if t["src"][0] == "out"]
+            staged = sum(1 for t in call if t["src"][0] == "stage")
+            if staged:
+                waits.append(("sg%d" % i, 16 * staged))
+            for t in call:
+                if "far" in t:
+                    t["late"] = (0, i, t["far"])
+            own[s].append((waits, call))
+        seqs.append([[t["blk"] for t in call] for call in calls])
+    prog = {}
+    for c in set(own) | set(fwd):
+        prog[c] = list(own.get(c, []))
+        for sem, ins, outs in fwd.get(c, []):
+            _deal(c, outs, topo)
+            prog[c].append(([(sem, sum(len(t["eng"]) for t in ins))], outs))
+    for c, calls in prog.items():
+        for _, call in calls:
+            for t in call:
+                if "late" in t:
+                    arrive[cores.index(t["to"])][int(t["sem"][1:])] = (t["late"], t["dst"][0], len(t["eng"]))
+    return prog, seqs, arrive
+
+
+def _ap(T, spec):
+    name, k = spec
+    if name in ("out", "land"):
+        return T[name][:, TK * k:TK * (k + 1)]
+    return T[name][k]
+
+
+def _send(g, T, topo, calls):
+    total = 0
+    for waits, call in calls:
+        for sem, count in waits:
+            g.wait_ge(T.sem[sem], count)
+        trs = []
+        for t in call:
+            rid, pid, _ = topo.addr(t["to"])
+            total += len(t["eng"])
+            trs.append((rid, pid, sum(1 << b for b in t["eng"]), t))
+        if len(trs) == 1:
+            rid, pid, mask, t = trs[0]
+            g.remote_dma(out_ap=_ap(T, t["dst"]), in_ap=_ap(T, t["src"]), remote_sem=T.sem[t["sem"]],
+                         local_sem=T.sem.sent, pid=pid, routing_id=rid, dma_engine_mask=mask)
+        else:
+            g.remote_dma_fused([RemoteDMATransfer(dst_ids=[DstId(rid=rid, pnc=pid)], dma_engine_mask=mask,
+                                                  remote_sem=T.sem[t["sem"]], src=_ap(T, t["src"]),
+                                                  dst=_ap(T, t["dst"])) for rid, pid, mask, t in trs],
+                               local_sem=T.sem.sent)
+    if total:
+        g.wait_ge(T.sem.sent, total)
+
+
+def _runs(tiles):
+    runs = []
+    for k in sorted(tiles):
+        if runs and runs[-1][1] == k:
+            runs[-1][1] = k + 1
+        else:
+            runs.append([k, k + 1])
+    return runs
+
+
+def rank_program(g, core, T, topo):
+    cores = list(T.cores)
+    prog, seqs, arrive = _plan(cores, topo)
+    rank = T.rank_of(core)
+    if rank is None:
+        if core in prog:
+            _send(g, T, topo, prog[core])
+        return
+
+    calls = seqs[rank]
+    lead = list(calls[0])
+    if topo.chip(cores[lead[0]]) == topo.chip(core):
+        lead.append(rank)
+    first = [N * t + r for t in range(KT) for r in lead] if SPLIT_LOAD else list(range(KT * N))
+    rest = [k for k in range(KT * N) if k not in first]
+    queues = (g.sync, g.scalar)
+    g.sync.dma_start(T.xs[:], T.x[:]).then_inc(T.sem.ldx, 16)
+    turn, counts = 1, []
+    for sem, tiles in ((T.sem.ldw0, first), (T.sem.ldw1, rest)):
+        runs = _runs(tiles)
+        counts.append(16 * len(runs))
+        for a, b in runs:
+            queues[turn % 2].dma_start(T.ws[:, FB * a:FB * b], T.w[:, FB * a:FB * b]).then_inc(sem, 16)
+            turn += 1
+
+    order = [(r, i) for i, call in enumerate(calls) for r in call] + [(rank, None)]
+    staged = {t["blk"] for _, call in prog[core] for t in call if t["src"][0] == "stage"}
+    g.tensor.wait_ge(T.sem.ldx, 16)
+    g.tensor.wait_ge(T.sem.ldw0, counts[0])
+    for i, (r, call) in enumerate(order):
+        if i == len(calls[0]) and counts[1]:
+            g.tensor.wait_ge(T.sem.ldw1, counts[1])
+        ps = T["ps%d" % i]
+        blk = T.out[:, TK * r:TK * (r + 1)]
+        for t in range(KT):
+            k = N * t + r
+            mm = g.tensor.matmul(ps[:, 0:TK], T.ws[:, FB * k:FB * (k + 1)], T.xs[:, TK * t:TK * (t + 1)],
+                                 t == 0, t == KT - 1)
+        mm.then_inc(T.sem["mm%d" % i], 1)
+        g.vector.wait_ge(T.sem["mm%d" % i], 1)
+        g.vector.tensor_copy(blk, ps[:, 0:TK]).then_inc(T.sem["cp%d" % i], 1)
+        if r in staged or r == rank:
+            q = queues[i % 2]
+            q.wait_ge(T.sem["cp%d" % i], 1)
+            if r == rank:
+                q.dma_start(T.y[:, TK * r:TK * (r + 1)], blk).then_inc(T.sem.st, 16)
+            else:
+                q.dma_start(T.stage[r], blk).then_inc(T.sem["sg%d" % call], 16)
+
+    come = sorted(arrive[rank].items(), key=lambda kv: kv[1][0])
+    for i, (j, (_, where, count)) in enumerate(come):
+        q = queues[i % 2]
+        q.wait_ge(T.sem["a%d" % j], count)
+        q.dma_start(T.y[:, TK * j:TK * (j + 1)], _ap(T, (where, j))).then_inc(T.sem.st, 16)
+
+    _send(g, T, topo, prog[core])
+    g.wait_ge(T.sem.st, 16 * N)

@@ -4,31 +4,31 @@ N, KT, FB, TK = 6, 2, 128, 256
 SIM_CORES = 80
 SLOTS = 4
 
-RELAY = "helper"
-FAR_VIA_PLANE = False
-STAGE = False
-HOME_FIRST = False
-SPLIT_LOAD = True
 N_HOP1 = 4
 N_FWD = 4
 N_HOME = 8
 N_DIRECT = 4
-SPREAD = True
+WIDE = False
+VIA_IDLE = True
+LEAD = 64
+WIDTHS = (LEAD, TK - LEAD, TK)
+NP = 8
 
 SCRATCH = {
     "xs": ("sbuf", [128, KT * TK], "bfloat16"),
     "ws": ("sbuf", [128, KT * N * FB], "bfloat16"),
     "out": ("sbuf", [128, N * TK], "bfloat16"),
     "land": ("sbuf", [128, N * TK], "bfloat16"),
-    "stage": ("dram", [N, 128, TK], "bfloat16"),
-    "relay": ("dram", [SLOTS, 128, TK], "bfloat16"),
-    "dland": ("dram", [N, 128, TK], "bfloat16"),
 }
-for _i in range(N):
+for _w in WIDTHS:
+    SCRATCH["relay%d" % _w] = ("dram", [SLOTS, 128, _w], "bfloat16")
+    SCRATCH["dland%d" % _w] = ("dram", [N, 128, _w], "bfloat16")
+for _i in range(NP):
     SCRATCH["ps%d" % _i] = ("psum", [128, 512], "float32")
 
-SEMAPHORES = (["ldx", "ldw0", "ldw1", "sent", "st"] + ["mm%d" % i for i in range(N)] + ["cp%d" % i for i in range(N)]
-              + ["sg%d" % i for i in range(4)] + ["a%d" % i for i in range(N)] + ["r%d" % i for i in range(SLOTS)])
+SEMAPHORES = (["ld0", "ld1", "sent", "st"] + ["lg%d" % i for i in range(1, 4)] + ["mm%d" % i for i in range(NP)]
+              + ["cp%d" % i for i in range(NP)] + ["a%d" % i for i in range(N)] + ["b%d" % i for i in range(N)]
+              + ["r%d" % i for i in range(SLOTS)])
 
 
 def _bits(m):
@@ -51,34 +51,28 @@ def _engine_sets(core, topo):
     return _bits(every), _bits(some & ~every)
 
 
-def _relays(s, dsts, cores, topo, links, nth):
+def _relays(s, dsts, cores, topo, far):
     cs, cd = topo.chip(s), topo.chip(dsts[0])
-
-    def fits(h):
-        return h != s and topo.may_write(s, h) and all(topo.may_write(h, d) for d in dsts)
-
-    if FAR_VIA_PLANE and links == 2:
-        got = [h for h in range(SIM_CORES) if h not in cores and fits(h) and topo.same_plane(cs, topo.chip(h))
-               and topo.mates(topo.chip(h), cd) and topo.die(h) == topo.die(s)]
-        if got:
-            return got
-    if RELAY == "sibling" or (RELAY == "mixed" and nth > 0):
-        got = [h for h in cores if topo.chip(h) == cs and fits(h)]
-        if got:
-            return got
-    return [h for h in range(SIM_CORES) if h not in cores and fits(h) and topo.chip(h) == cs
-            and topo.die(h) == topo.die(s)]
+    busy = {topo.chip(c) for c in cores}
+    got = [h for h in range(SIM_CORES) if h not in cores and topo.may_write(s, h)
+           and all(topo.may_write(h, d) for d in dsts)]
+    there = [h for h in got if VIA_IDLE and far and topo.chip(h) not in busy and topo.same_plane(cs, topo.chip(h))
+             and topo.mates(topo.chip(h), cd)]
+    got = there or [h for h in got if topo.chip(h) == cs]
+    mine = [h for h in got if topo.die(h) == topo.die(s)]
+    other = [h for h in got if topo.die(h) != topo.die(s)]
+    return [grp for grp in (mine, other) if grp]
 
 
 def _deal(core, call, topo):
     caps = {"hop1": N_HOP1, "fwd": N_FWD, "home": N_HOME, "direct": N_DIRECT}
     narrow, upper = _engine_sets(core, topo)
-    for pool, inside in ((upper or narrow, True), (narrow, False)):
+    stays = all(topo.chip(t["to"]) == topo.chip(core) for t in call)
+    for pool, inside in ((upper + narrow if WIDE and stays else (upper or narrow), True), (narrow, False)):
         part = [t for t in call if (topo.chip(t["to"]) == topo.chip(core)) == inside]
         if not part:
             continue
-        if SPREAD:
-            pool = pool[0::2] + pool[1::2]
+        pool = pool[0::2] + pool[1::2]
         n = _pow2(len(pool) // len(part))
         at = 0
         for t in part:
@@ -106,56 +100,42 @@ def _plan(cores, topo):
 
         away = sorted(groups.items(), key=lambda kv: (free(kv[1]), -links(kv[0])))
         calls = []
-        homes = [dict(to=cores[r], src=("out", r), dst=("land", j), sem="a%d" % j, kind="home", blk=r, far=0)
-                 for r in home]
-        early = HOME_FIRST and homes and all(free(rs) for _, rs in away)
-        if early:
-            calls.append(homes)
+        homes = [dict(to=cores[r], src=("out", r, 0, TK), dst=("land", j, 0, TK), sem="a%d" % j, kind="home", blk=r,
+                      far=0) for r in home]
         for ch, rs in away:
-            call = []
             if free(rs):
-                long = STAGE is True or (STAGE == "later" and len(calls) > 0)
-                for r in rs:
-                    call.append(dict(to=cores[r], src=("stage" if long else "out", r),
-                                     dst=("dland" if long else "land", j), sem="a%d" % j, kind="direct", blk=r,
-                                     far=links(ch)))
-            else:
-                hs = _relays(s, [cores[r] for r in rs], cores, topo, links(ch), len(calls))
-                batch = {}
+                calls.append([dict(to=cores[r], src=("out", r, 0, TK), dst=("land", j, 0, TK), sem="a%d" % j,
+                                   kind="direct", blk=r, far=links(ch)) for r in rs])
+                continue
+            hs = _relays(s, [cores[r] for r in rs], cores, topo, links(ch) == 2)
+            cuts = [(0, LEAD, "b"), (LEAD, TK, "a")] if LEAD and not calls else [(0, TK, "a")]
+            for c0, c1, letter in cuts:
+                call = []
                 for i, r in enumerate(rs):
-                    h = hs[i % len(hs)]
+                    h = hs[i % len(hs)][0]
                     k = slots.get(h, 0)
                     slots[h] = k + 1
-                    if h not in batch:
-                        batch[h] = ("r%d" % k, [], [])
-                    sem, ins, outs = batch[h]
-                    t = dict(to=h, src=("out", r), dst=("relay", k), sem=sem, kind="hop1", blk=r)
+                    t = dict(to=h, src=("out", r, c0, c1), dst=("relay%d" % (c1 - c0), k), sem="r%d" % k, kind="hop1",
+                             blk=r)
                     call.append(t)
-                    ins.append(t)
-                    outs.append(dict(to=cores[r], src=("relay", k), dst=("dland", j), sem="a%d" % j, kind="fwd",
-                                     blk=r, late=(1, len(calls), links(ch))))
-                for h, b in batch.items():
-                    fwd.setdefault(h, []).append(b)
-            calls.append(call)
-        if not early:
-            for t in homes:
-                if calls and all(topo.chip(u["to"]) != cs for u in calls[-1]):
-                    calls[-1].append(t)
-                else:
-                    calls.append([t])
-        pos = {t["blk"]: i for i, t in enumerate(t for call in calls for t in call)}
+                    fwd.setdefault(h, []).append(("r%d" % k, [t], [dict(
+                        to=cores[r], src=("relay%d" % (c1 - c0), k), dst=("dland%d" % (c1 - c0), j),
+                        sem="%s%d" % (letter, j), kind="fwd", blk=r, cols=(c0, c1),
+                        late=(1, len(calls), links(ch)))]))
+                calls.append(call)
+        if homes:
+            calls.append(homes)
+        pos = {t["src"][1:3]: i for i, t in enumerate(t for call in calls for t in call)}
         own[s] = []
         for i, call in enumerate(calls):
             _deal(s, call, topo)
-            waits = [("cp%d" % pos[t["blk"]], 1) for t in call if t["src"][0] == "out"]
-            staged = sum(1 for t in call if t["src"][0] == "stage")
-            if staged:
-                waits.append(("sg%d" % i, 16 * staged))
+            waits = [("cp%d" % pos[t["src"][1:3]], 1) for t in call]
             for t in call:
                 if "far" in t:
                     t["late"] = (0, i, t["far"])
+                    t["cols"] = (0, TK)
             own[s].append((waits, call))
-        seqs.append([[t["blk"] for t in call] for call in calls])
+        seqs.append([[t["src"][1:] for t in call] for call in calls])
     prog = {}
     for c in set(own) | set(fwd):
         prog[c] = list(own.get(c, []))
@@ -166,15 +146,15 @@ def _plan(cores, topo):
         for _, call in calls:
             for t in call:
                 if "late" in t:
-                    arrive[cores.index(t["to"])][int(t["sem"][1:])] = (t["late"], t["dst"][0], len(t["eng"]))
+                    arrive[cores.index(t["to"])][t["sem"]] = (t["late"], t["dst"], len(t["eng"]), t["cols"])
     return prog, seqs, arrive
 
 
 def _ap(T, spec):
-    name, k = spec
-    if name in ("out", "land"):
-        return T[name][:, TK * k:TK * (k + 1)]
-    return T[name][k]
+    if len(spec) == 4:
+        name, k, c0, c1 = spec
+        return T[name][:, TK * k + c0:TK * k + c1]
+    return T[spec[0]][spec[1]]
 
 
 def _send(g, T, topo, calls):
@@ -220,50 +200,65 @@ def rank_program(g, core, T, topo):
         return
 
     calls = seqs[rank]
-    lead = list(calls[0])
-    if topo.chip(cores[lead[0]]) == topo.chip(core):
-        lead.append(rank)
-    first = [N * t + r for t in range(KT) for r in lead] if SPLIT_LOAD else list(range(KT * N))
-    rest = [k for k in range(KT * N) if k not in first]
+    pieces = [p for call in calls for p in call] + [(rank, 0, TK)]
+    groups = []
+    for call in calls:
+        new = sorted({p[0] for p in call} - {r for grp in groups for r in grp})
+        if new:
+            groups.append(new)
+    groups[-1].append(rank)
     queues = (g.sync, g.scalar)
-    g.sync.dma_start(T.xs[:], T.x[:]).then_inc(T.sem.ldx, 16)
-    turn, counts = 1, []
-    for sem, tiles in ((T.sem.ldw0, first), (T.sem.ldw1, rest)):
-        runs = _runs(tiles)
-        counts.append(16 * len(runs))
+    need = []
+    for t in range(KT):
+        g.sync.dma_start(T.xs[:, TK * t:TK * (t + 1)], T.x[:, TK * t:TK * (t + 1)]).then_inc(T.sem["ld%d" % t], 16)
+        runs = _runs([N * t + r for r in groups[0]])
         for a, b in runs:
-            queues[turn % 2].dma_start(T.ws[:, FB * a:FB * b], T.w[:, FB * a:FB * b]).then_inc(sem, 16)
-            turn += 1
+            g.scalar.dma_start(T.ws[:, FB * a:FB * b], T.w[:, FB * a:FB * b]).then_inc(T.sem["ld%d" % t], 16)
+        need.append(16 * (1 + len(runs)))
+    turn = 0
+    for n, grp in enumerate(groups):
+        if n:
+            runs = _runs([N * t + r for t in range(KT) for r in grp])
+            for a, b in runs:
+                queues[turn % 2].dma_start(T.ws[:, FB * a:FB * b], T.w[:, FB * a:FB * b]).then_inc(T.sem["lg%d" % n], 16)
+                turn += 1
+            need.append(16 * len(runs))
 
-    order = [(r, i) for i, call in enumerate(calls) for r in call] + [(rank, None)]
-    staged = {t["blk"] for _, call in prog[core] for t in call if t["src"][0] == "stage"}
-    g.tensor.wait_ge(T.sem.ldx, 16)
-    g.tensor.wait_ge(T.sem.ldw0, counts[0])
-    for i, (r, call) in enumerate(order):
-        if i == len(calls[0]) and counts[1]:
-            g.tensor.wait_ge(T.sem.ldw1, counts[1])
-        ps = T["ps%d" % i]
-        blk = T.out[:, TK * r:TK * (r + 1)]
-        for t in range(KT):
-            k = N * t + r
-            mm = g.tensor.matmul(ps[:, 0:TK], T.ws[:, FB * k:FB * (k + 1)], T.xs[:, TK * t:TK * (t + 1)],
-                                 t == 0, t == KT - 1)
-        mm.then_inc(T.sem["mm%d" % i], 1)
+    def mult(i, t):
+        r, c0, c1 = pieces[i]
+        k = N * t + r
+        mm = g.tensor.matmul(T["ps%d" % i][:, 0:c1 - c0], T.ws[:, FB * k:FB * (k + 1)],
+                             T.xs[:, TK * t + c0:TK * t + c1], t == 0, t == KT - 1)
+        if t == KT - 1:
+            mm.then_inc(T.sem["mm%d" % i], 1)
+
+    for n, grp in enumerate(groups):
+        mine = [i for i, p in enumerate(pieces) if p[0] in grp]
+        if n == 0:
+            for t in range(KT):
+                g.tensor.wait_ge(T.sem["ld%d" % t], need[t])
+                for i in mine:
+                    mult(i, t)
+        else:
+            g.tensor.wait_ge(T.sem["lg%d" % n], need[KT + n - 1])
+            for i in mine:
+                for t in range(KT):
+                    mult(i, t)
+    for i, (r, c0, c1) in enumerate(pieces):
+        blk = T.out[:, TK * r + c0:TK * r + c1]
         g.vector.wait_ge(T.sem["mm%d" % i], 1)
-        g.vector.tensor_copy(blk, ps[:, 0:TK]).then_inc(T.sem["cp%d" % i], 1)
-        if r in staged or r == rank:
+        g.vector.tensor_copy(blk, T["ps%d" % i][:, 0:c1 - c0]).then_inc(T.sem["cp%d" % i], 1)
+        if r == rank:
             q = queues[i % 2]
             q.wait_ge(T.sem["cp%d" % i], 1)
-            if r == rank:
-                q.dma_start(T.y[:, TK * r:TK * (r + 1)], blk).then_inc(T.sem.st, 16)
-            else:
-                q.dma_start(T.stage[r], blk).then_inc(T.sem["sg%d" % call], 16)
+            q.dma_start(T.y[:, TK * r:TK * (r + 1)], blk).then_inc(T.sem.st, 16)
 
     come = sorted(arrive[rank].items(), key=lambda kv: kv[1][0])
-    for i, (j, (_, where, count)) in enumerate(come):
+    for i, (sem, (_, where, count, (c0, c1))) in enumerate(come):
+        j = int(sem[1:])
         q = queues[i % 2]
-        q.wait_ge(T.sem["a%d" % j], count)
-        q.dma_start(T.y[:, TK * j:TK * (j + 1)], _ap(T, (where, j))).then_inc(T.sem.st, 16)
+        q.wait_ge(T.sem[sem], count)
+        q.dma_start(T.y[:, TK * j + c0:TK * j + c1], _ap(T, where)).then_inc(T.sem.st, 16)
 
     _send(g, T, topo, prog[core])
-    g.wait_ge(T.sem.st, 16 * N)
+    g.wait_ge(T.sem.st, 16 * (1 + len(come)))

from concourse.bass import DstId, RemoteDMATransfer

N, KT, FB, TK = 6, 2, 128, 256
SIM_CORES = 80
SLOTS = 4

N_HOP1 = 4
N_FWD = 4
N_HOME = 8
N_DIRECT = 4
WIDE = False
VIA_IDLE = True
LEAD = 64
WIDTHS = (LEAD, TK - LEAD, TK)
NP = 8

SCRATCH = {
    "xs": ("sbuf", [128, KT * TK], "bfloat16"),
    "ws": ("sbuf", [128, KT * N * FB], "bfloat16"),
    "out": ("sbuf", [128, N * TK], "bfloat16"),
    "land": ("sbuf", [128, N * TK], "bfloat16"),
}
for _w in WIDTHS:
    SCRATCH["relay%d" % _w] = ("dram", [SLOTS, 128, _w], "bfloat16")
    SCRATCH["dland%d" % _w] = ("dram", [N, 128, _w], "bfloat16")
for _i in range(NP):
    SCRATCH["ps%d" % _i] = ("psum", [128, 512], "float32")

SEMAPHORES = (["ld0", "ld1", "sent", "st"] + ["lg%d" % i for i in range(1, 4)] + ["mm%d" % i for i in range(NP)]
              + ["cp%d" % i for i in range(NP)] + ["a%d" % i for i in range(N)] + ["b%d" % i for i in range(N)]
              + ["r%d" % i for i in range(SLOTS)])


def _bits(m):
    return [b for b in range(m.bit_length()) if (m >> b) & 1]


def _pow2(n):
    p = 1
    while p * 2 <= n:
        p *= 2
    return p


def _engine_sets(core, topo):
    every, some = ~0, 0
    for c in range(SIM_CORES):
        if c != core:
            every &= topo.mask(core, c)
            some |= topo.mask(core, c)
    return _bits(every), _bits(some & ~every)


def _relays(s, dsts, cores, topo, far):
    cs, cd = topo.chip(s), topo.chip(dsts[0])
    busy = {topo.chip(c) for c in cores}
    got = [h for h in range(SIM_CORES) if h not in cores and topo.may_write(s, h)
           and all(topo.may_write(h, d) for d in dsts)]
    there = [h for h in got if VIA_IDLE and far and topo.chip(h) not in busy and topo.same_plane(cs, topo.chip(h))
             and topo.mates(topo.chip(h), cd)]
    got = there or [h for h in got if topo.chip(h) == cs]
    mine = [h for h in got if topo.die(h) == topo.die(s)]
    other = [h for h in got if topo.die(h) != topo.die(s)]
    return [grp for grp in (mine, other) if grp]


def _deal(core, call, topo):
    caps = {"hop1": N_HOP1, "fwd": N_FWD, "home": N_HOME, "direct": N_DIRECT}
    narrow, upper = _engine_sets(core, topo)
    stays = all(topo.chip(t["to"]) == topo.chip(core) for t in call)
    for pool, inside in ((upper + narrow if WIDE and stays else (upper or narrow), True), (narrow, False)):
        part = [t for t in call if (topo.chip(t["to"]) == topo.chip(core)) == inside]
        if not part:
            continue
        pool = pool[0::2] + pool[1::2]
        n = _pow2(len(pool) // len(part))
        at = 0
        for t in part:
            k = min(n, caps[t["kind"]])
            t["eng"] = pool[at:at + k]
            at += k


def _plan(cores, topo):
    own, fwd, seqs, slots = {}, {}, [], {}
    arrive = [dict() for _ in cores]
    for j, s in enumerate(cores):
        cs = topo.chip(s)
        groups = {}
        for r, d in enumerate(cores):
            if r != j:
                groups.setdefault(topo.chip(d), []).append(r)
        home = groups.pop(cs, [])

        def links(ch):
            return 1 if (topo.mates(cs, ch) or topo.same_plane(cs, ch)) else 2

        def free(rs):
            return all(topo.may_write(s, cores[r]) for r in rs)

        away = sorted(groups.items(), key=lambda kv: (free(kv[1]), -links(kv[0])))
        calls = []
        homes = [dict(to=cores[r], src=("out", r, 0, TK), dst=("land", j, 0, TK), sem="a%d" % j, kind="home", blk=r,
                      far=0) for r in home]
        for ch, rs in away:
            if free(rs):
                calls.append([dict(to=cores[r], src=("out", r, 0, TK), dst=("land", j, 0, TK), sem="a%d" % j,
                                   kind="direct", blk=r, far=links(ch)) for r in rs])
                continue
            hs = _relays(s, [cores[r] for r in rs], cores, topo, links(ch) == 2)
            cuts = [(0, LEAD, "b"), (LEAD, TK, "a")] if LEAD and not calls else [(0, TK, "a")]
            for c0, c1, letter in cuts:
                call = []
                for i, r in enumerate(rs):
                    h = hs[i % len(hs)][0]
                    k = slots.get(h, 0)
                    slots[h] = k + 1
                    t = dict(to=h, src=("out", r, c0, c1), dst=("relay%d" % (c1 - c0), k), sem="r%d" % k, kind="hop1",
                             blk=r)
                    call.append(t)
                    fwd.setdefault(h, []).append(("r%d" % k, [t], [dict(
                        to=cores[r], src=("relay%d" % (c1 - c0), k), dst=("dland%d" % (c1 - c0), j),
                        sem="%s%d" % (letter, j), kind="fwd", blk=r, cols=(c0, c1),
                        late=(1, len(calls), links(ch)))]))
                calls.append(call)
        if homes:
            calls.append(homes)
        pos = {t["src"][1:3]: i for i, t in enumerate(t for call in calls for t in call)}
        own[s] = []
        for i, call in enumerate(calls):
            _deal(s, call, topo)
            waits = [("cp%d" % pos[t["src"][1:3]], 1) for t in call]
            for t in call:
                if "far" in t:
                    t["late"] = (0, i, t["far"])
                    t["cols"] = (0, TK)
            own[s].append((waits, call))
        seqs.append([[t["src"][1:] for t in call] for call in calls])
    prog = {}
    for c in set(own) | set(fwd):
        prog[c] = list(own.get(c, []))
        for sem, ins, outs in fwd.get(c, []):
            _deal(c, outs, topo)
            prog[c].append(([(sem, sum(len(t["eng"]) for t in ins))], outs))
    for c, calls in prog.items():
        for _, call in calls:
            for t in call:
                if "late" in t:
                    arrive[cores.index(t["to"])][t["sem"]] = (t["late"], t["dst"], len(t["eng"]), t["cols"])
    return prog, seqs, arrive


def _ap(T, spec):
    if len(spec) == 4:
        name, k, c0, c1 = spec
        return T[name][:, TK * k + c0:TK * k + c1]
    return T[spec[0]][spec[1]]


def _send(g, T, topo, calls):
    total = 0
    for waits, call in calls:
        for sem, count in waits:
            g.wait_ge(T.sem[sem], count)
        trs = []
        for t in call:
            rid, pid, _ = topo.addr(t["to"])
            total += len(t["eng"])
            trs.append((rid, pid, sum(1 << b for b in t["eng"]), t))
        if len(trs) == 1:
            rid, pid, mask, t = trs[0]
            g.remote_dma(out_ap=_ap(T, t["dst"]), in_ap=_ap(T, t["src"]), remote_sem=T.sem[t["sem"]],
                         local_sem=T.sem.sent, pid=pid, routing_id=rid, dma_engine_mask=mask)
        else:
            g.remote_dma_fused([RemoteDMATransfer(dst_ids=[DstId(rid=rid, pnc=pid)], dma_engine_mask=mask,
                                                  remote_sem=T.sem[t["sem"]], src=_ap(T, t["src"]),
                                                  dst=_ap(T, t["dst"])) for rid, pid, mask, t in trs],
                               local_sem=T.sem.sent)
    if total:
        g.wait_ge(T.sem.sent, total)


def _runs(tiles):
    runs = []
    for k in sorted(tiles):
        if runs and runs[-1][1] == k:
            runs[-1][1] = k + 1
        else:
            runs.append([k, k + 1])
    return runs


def rank_program(g, core, T, topo):
    cores = list(T.cores)
    prog, seqs, arrive = _plan(cores, topo)
    rank = T.rank_of(core)
    if rank is None:
        if core in prog:
            _send(g, T, topo, prog[core])
        return

    calls = seqs[rank]
    pieces = [p for call in calls for p in call] + [(rank, 0, TK)]
    groups = []
    for call in calls:
        new = sorted({p[0] for p in call} - {r for grp in groups for r in grp})
        if new:
            groups.append(new)
    groups[-1].append(rank)
    queues = (g.sync, g.scalar)
    need = []
    for t in range(KT):
        g.sync.dma_start(T.xs[:, TK * t:TK * (t + 1)], T.x[:, TK * t:TK * (t + 1)]).then_inc(T.sem["ld%d" % t], 16)
        runs = _runs([N * t + r for r in groups[0]])
        for a, b in runs:
            g.scalar.dma_start(T.ws[:, FB * a:FB * b], T.w[:, FB * a:FB * b]).then_inc(T.sem["ld%d" % t], 16)
        need.append(16 * (1 + len(runs)))
    turn = 0
    for n, grp in enumerate(groups):
        if n:
            runs = _runs([N * t + r for t in range(KT) for r in grp])
            for a, b in runs:
                queues[turn % 2].dma_start(T.ws[:, FB * a:FB * b], T.w[:, FB * a:FB * b]).then_inc(T.sem["lg%d" % n], 16)
                turn += 1
            need.append(16 * len(runs))

    def mult(i, t):
        r, c0, c1 = pieces[i]
        k = N * t + r
        mm = g.tensor.matmul(T["ps%d" % i][:, 0:c1 - c0], T.ws[:, FB * k:FB * (k + 1)],
                             T.xs[:, TK * t + c0:TK * t + c1], t == 0, t == KT - 1)
        if t == KT - 1:
            mm.then_inc(T.sem["mm%d" % i], 1)

    for n, grp in enumerate(groups):
        mine = [i for i, p in enumerate(pieces) if p[0] in grp]
        if n == 0:
            for t in range(KT):
                g.tensor.wait_ge(T.sem["ld%d" % t], need[t])
                for i in mine:
                    mult(i, t)
        else:
            g.tensor.wait_ge(T.sem["lg%d" % n], need[KT + n - 1])
            for i in mine:
                for t in range(KT):
                    mult(i, t)
    for i, (r, c0, c1) in enumerate(pieces):
        blk = T.out[:, TK * r + c0:TK * r + c1]
        g.vector.wait_ge(T.sem["mm%d" % i], 1)
        g.vector.tensor_copy(blk, T["ps%d" % i][:, 0:c1 - c0]).then_inc(T.sem["cp%d" % i], 1)
        if r == rank:
            q = queues[i % 2]
            q.wait_ge(T.sem["cp%d" % i], 1)
            q.dma_start(T.y[:, TK * r:TK * (r + 1)], blk).then_inc(T.sem.st, 16)

    come = sorted(arrive[rank].items(), key=lambda kv: kv[1][0])
    for i, (sem, (_, where, count, (c0, c1))) in enumerate(come):
        j = int(sem[1:])
        q = queues[i % 2]
        q.wait_ge(T.sem[sem], count)
        q.dma_start(T.y[:, TK * j + c0:TK * j + c1], _ap(T, where)).then_inc(T.sem.st, 16)

    _send(g, T, topo, prog[core])
    g.wait_ge(T.sem.st, 16 * (1 + len(come)))
